import numpy as np
import ml_dtypes


def mxq(x, axis, fmt="e4m3"):
    dtype, down = {"e4m3": (ml_dtypes.float8_e4m3fn, 7), "e5m2": (ml_dtypes.float8_e5m2, 14)}[fmt]
    v = np.moveaxis(np.asarray(x, np.float32).astype(ml_dtypes.bfloat16).astype(np.float64), axis, -1)
    blocks = v.reshape(v.shape[:-1] + (-1, 32))
    amax = np.abs(blocks).max(-1, keepdims=True)
    byte = np.maximum(np.where(amax > 0, np.frexp(amax)[1] - 1 + 127, 0) - down, 1)
    scale = np.exp2(byte - 127.0)
    codes = (blocks / scale).astype(np.float32).astype(dtype).astype(np.float64)
    return np.moveaxis((codes * scale).reshape(v.shape), -1, axis)


WIDE = False


def mx_kscale(k):
    if not WIDE:
        return np.ones(k)
    levels = np.array([10, -10, 5, -5, 0])
    if k % 512:
        return np.exp2(np.random.permutation(np.resize(levels, k // 32))).repeat(32)
    a = np.empty((k // 512, 16))
    for p in range(k // 512):
        a[p, :8] = np.random.permutation(np.resize(levels, 8))
        for g in range(8):
            far = levels[np.abs(levels - a[p, g]) >= 10]
            a[p, g + 8] = far[np.random.randint(len(far))]
    return np.exp2(a.ravel()).repeat(32)


BF16 = ml_dtypes.bfloat16


def bf(x):
    return np.asarray(x, np.float32).astype(BF16)


def f64(x):
    return np.asarray(x).astype(np.float64)


E2M1 = np.array([0.0, 0.5, 1.0, 1.5, 2.0, 3.0, 4.0, 6.0, -0.0, -0.5, -1.0, -1.5, -2.0, -3.0, -4.0, -6.0])


def pack_weight(w, fmt):
    k, n = w.shape
    w = f64(bf(w)).reshape(k // 32, 32, n)
    amax = np.abs(w).max(1)
    if fmt == "e4m3":
        byte = np.frexp(amax)[1] - 1 + 127 - 7
    else:
        mant, ex = np.frexp(amax / 6.0)
        byte = np.where(mant > 0.5, ex, ex - 1) + 127
    byte = np.clip(np.where(amax > 0, byte, 1), 1, 254)
    scaled = (w * np.exp2(127.0 - byte)[:, None, :]).reshape(k, n).astype(np.float32)
    by_word = np.ascontiguousarray(scaled.reshape(k // 512, 128, 4, n).transpose(0, 1, 3, 2))
    if fmt == "e4m3":
        words = by_word.astype(ml_dtypes.float8_e4m3fn).view(np.uint8)
    else:
        c = by_word.astype(ml_dtypes.float4_e2m1fn).view(np.uint8) & 0xF
        words = c[..., 0::2] | (c[..., 1::2] << 4)
    return np.ascontiguousarray(words), np.ascontiguousarray(byte.astype(np.uint8).reshape(k // 512, 16, n))


def unpack_weight(words, scales, fmt):
    g, p, n, _ = words.shape
    if fmt == "e4m3":
        vals = np.ascontiguousarray(words).view(ml_dtypes.float8_e4m3fn).astype(np.float64)
    else:
        nib = np.empty((g, p, n, 4), np.uint8)
        nib[..., 0::2] = words & 0xF
        nib[..., 1::2] = words >> 4
        vals = E2M1[nib]
    vals = vals * np.repeat(np.exp2(scales.astype(np.float64) - 127.0), 8, axis=1)[..., None]
    return vals.transpose(0, 1, 3, 2).reshape(g * 512, n)
def pack4(w):
    words, scales = pack_weight(w, "e2m1")
    return words.reshape(words.shape[0], 128, -1), scales


def unpack4(words, scales):
    return unpack_weight(words.reshape(words.shape[0], 128, -1, 2), scales, "e2m1")


M, K, D, R, C = 2048, 1536, 1024, 1024, 512


def setup_inputs():
    a, b, c = mx_kscale(K), mx_kscale(D), mx_kscale(R)
    x = bf(np.random.standard_normal((M, K)) * a)
    w = bf(np.random.standard_normal((K, D)) / np.sqrt(K) / a[:, None] * b)
    u = np.random.standard_normal((R, D)) / np.sqrt(R) * c[:, None] / b
    v = np.random.standard_normal((R, C)) * np.sqrt(2 / D) / c[:, None]
    u_words, u_scales = pack4(u)
    v_words, v_scales = pack4(v)
    y = bf(np.sign(np.random.standard_normal((M, C))))
    return {"x": x, "w": w,
            "u_words": u_words, "u_scales": u_scales,
            "v_words": v_words, "v_scales": v_scales,
            "y": y}


def reference(x, w, u_words, u_scales, v_words, v_scales, y):
    feat = np.maximum(mxq(f64(x), 1, "e4m3") @ mxq(f64(w), 0, "e4m3"), 0)
    head = unpack4(u_words, u_scales).T @ unpack4(v_words, v_scales)
    err = (mxq(feat, 1, "e4m3") @ mxq(head, 0, "e4m3")) - f64(y)
    score = np.mean(err * err, axis=1)
    return err, score

@@ -1,0 +1,267 @@
+from contextlib import ExitStack
+
+import concourse.mybir as mybir
+from concourse.masks import make_identity
+
+M, K, D, R, C = 2048, 1536, 1024, 1024, 512
+FLOPS = 2 * (M * K * D + D * R * C + M * D * C)
+
+F32 = mybir.dt.float32
+BF16 = mybir.dt.bfloat16
+I32 = mybir.dt.int32
+U32 = mybir.dt.uint32
+U8 = mybir.dt.uint8
+FP8 = mybir.dt.float8_e4m3fn_x4
+FP4 = mybir.dt.float4_e2m1fn_x4
+COPY = mybir.ActivationFunctionType.Copy
+RELU = mybir.ActivationFunctionType.Relu
+SQUARE = mybir.ActivationFunctionType.Square
+SUB = mybir.AluOpType.subtract
+
+P = 128
+GX = K // 512
+GR = R // 512
+H = D // 512
+TILES = M // P
+PAIRS = TILES // 2
+
+
+def tile_el2n_pruning_score_s12_kernel(tc, x, w, u_words, u_scales, v_words, v_scales, y, out_0, out_1):
+    nc = tc.nc
+    with ExitStack() as ctx:
+        keep = ctx.enter_context(tc.tile_pool(name="keep", bufs=1))
+        work = ctx.enter_context(tc.tile_pool(name="work", bufs=3))
+        psum = ctx.enter_context(tc.psum_pool(name="psum", bufs=3))
+
+        u_plane = keep.tile([P, GR, D], U8, name="u_plane", align_bytes=64)
+        v_plane = keep.tile([P, GR, C], U8, name="v_plane", align_bytes=64)
+        nc.vector.memset(v_plane[:].bitcast(I32), 0)
+        nc.vector.memset(u_plane[:].bitcast(I32), 0)
+        warm = keep.tile([P, 1], F32, name="warm")
+        nc.vector.memset(warm[:], 0.0)
+        warm2 = keep.tile([P, 1], F32, name="warm2")
+        nc.scalar.activation(out=warm2[:], in_=warm[:], func=RELU)
+
+        u_raw = keep.tile([P, GR, 2 * D], U8, name="u_raw", align_bytes=64)
+        v_raw = keep.tile([P, GR, 2 * C], U8, name="v_raw", align_bytes=64)
+        nc.sync.dma_start(out=u_raw[:].bitcast(I32), in_=u_words.bitcast(I32).rearrange("g p n -> p g n"))
+        nc.sync.dma_start(out=v_raw[:].bitcast(I32), in_=v_words.bitcast(I32).rearrange("g p n -> p g n"))
+        us = u_scales.bitcast(I32).rearrange("g q n -> q g n")
+        vs = v_scales.bitcast(I32).rearrange("g q n -> q g n")
+        for q in range(4):
+            nc.scalar.dma_start(out=u_plane[32 * q : 32 * q + 4].bitcast(I32), in_=us[4 * q : 4 * q + 4])
+            nc.gpsimd.dma_start(out=v_plane[32 * q : 32 * q + 4].bitcast(I32), in_=vs[4 * q : 4 * q + 4])
+        ident = keep.tile([P, P], F32, name="ident")
+        make_identity(nc, ident[:])
+
+        x_rows = x.rearrange("(p i) k -> p i k", i=TILES)
+        y_rows = y.rearrange("(p i) c -> p i c", i=TILES)
+        out_rows = out_0.rearrange("(p i) c -> p i c", i=TILES)
+        w_rows = w.rearrange("(g p j) d -> g p j d", p=P, j=4)
+
+        x_raw = [keep.tile([P, 2, K], BF16, name=f"x_raw{n}", align_bytes=64) for n in range(PAIRS)]
+        y_sb = [keep.tile([P, 4, C], BF16, name=f"y_sb{n}", align_bytes=64) for n in range(TILES // 4)]
+        w_raw = [[keep.tile([P, 4, 512], BF16, name=f"w_raw{h}{g}", align_bytes=64) for g in range(GX)] for h in range(H)]
+
+        def load_w(h):
+            for g in range(GX):
+                nc.sync.dma_start(out=w_raw[h][g][:], in_=w_rows[g][:, :, 512 * h : 512 * h + 512])
+
+        def load_x(n):
+            nc.sync.dma_start(out=x_raw[n][:], in_=x_rows[:, 2 * n : 2 * n + 2, :])
+
+        def load_y(n):
+            nc.sync.dma_start(out=y_sb[n][:], in_=y_rows[:, 4 * n : 4 * n + 4, :])
+
+        load_x(0)
+        load_w(0)
+        load_w(1)
+        load_x(1)
+        load_x(2)
+        load_y(0)
+        load_x(3)
+        load_x(4)
+        load_y(1)
+        load_x(5)
+        load_x(6)
+        load_y(2)
+        load_x(7)
+        load_y(3)
+
+        u_codes = keep.tile([P, GR, 2 * D], U8, name="u_codes", align_bytes=64)
+        u_perm = keep.tile([P, GR, D], U8, name="u_perm", align_bytes=64)
+        for g in range(GR):
+            nc.vector.tensor_copy(
+                out=u_codes[:, g, :].bitcast(I32).rearrange("p (t q b) -> p t q b", t=4, b=4),
+                in_=u_raw[:, g, :].bitcast(I32).rearrange("p (q t b) -> p t q b", t=4, b=4),
+            )
+        for g in range(GR):
+            nc.vector.tensor_copy(
+                out=u_perm[:, g, :].bitcast(I32).rearrange("p (t q b) -> p t q b", t=4, b=2),
+                in_=u_plane[:, g, :].bitcast(I32).rearrange("p (q t b) -> p t q b", t=4, b=2),
+            )
+
+        head_bf = keep.tile([P, H, 4 * C], BF16, name="head_bf", align_bytes=64)
+        head_codes = keep.tile([P, H, C], U32, name="head_codes", align_bytes=64)
+        head_scales = keep.tile([P, H, C], U8, name="head_scales", align_bytes=64)
+        for h in range(H):
+            for cc in range(4):
+                acc = psum.tile([P, 4, P], F32, name="acc", tag="acc", bufs=3)
+                for t in range(4):
+                    col = 256 * t + 128 * h
+                    for g in range(GR):
+                        nc.tensor.matmul_mx(
+                            out=acc[:, t, :],
+                            lhsT=u_codes[:, g, 2 * col : 2 * col + 256].bitcast(FP4),
+                            lhsT_scale=u_perm[:, g, col : col + 128],
+                            rhs=v_raw[:, g, 256 * cc : 256 * cc + 256].bitcast(FP4),
+                            rhs_scale=v_plane[:, g, 128 * cc : 128 * cc + 128],
+                            start=(g == 0),
+                            stop=(g == GR - 1),
+                        )
+                dst = head_bf[:, h, 512 * cc : 512 * cc + 512].rearrange("p (c t) -> p c t", t=4)
+                src = acc[:].rearrange("p t c -> p c t")
+                if cc == 3:
+                    nc.vector.tensor_copy(out=dst, in_=src)
+                else:
+                    nc.scalar.copy(out=dst, in_=src)
+
+        w_bf = [[keep.tile([P, 2048], BF16, name=f"w_bf{h}{g}", align_bytes=64) for g in range(GX)] for h in range(H)]
+        w_codes = [[keep.tile([P, 512], U32, name=f"w_codes{h}{g}", align_bytes=64) for g in range(GX)] for h in range(H)]
+        w_scales = [[keep.tile([P, 512], U8, name=f"w_scales{h}{g}", align_bytes=64) for g in range(GX)] for h in range(H)]
+
+        def prep_w(h):
+            for g in range(GX):
+                src = w_raw[h][g][:].rearrange("p j (q t r) -> p t q r j", t=4, r=8)
+                dst = w_bf[h][g][:].rearrange("p (t q r j) -> p t q r j", t=4, r=8, j=4)
+                for t in range(4):
+                    if t == 3:
+                        nc.scalar.copy(out=dst[:, t], in_=src[:, t])
+                    else:
+                        nc.vector.tensor_copy(out=dst[:, t], in_=src[:, t])
+                nc.vector.quantize_mx(out=w_codes[h][g][:].bitcast(FP8), scales=w_scales[h][g][:], in_=w_bf[h][g][:])
+
+        x_split = {}
+        x_bf = {}
+        x_codes = {}
+        x_scales = {}
+
+        def split_x(n):
+            xs = work.tile([P, 2, 2, K // 4], F32, name="x_split", align_bytes=64)
+            nc.vector.tensor_copy(out=xs[:], in_=x_raw[n][:].bitcast(F32).rearrange("p i (w u) -> p i u w", u=2))
+            x_split[n] = xs
+
+        def turn_x(n):
+            xb = work.tile([P, 6 * 512], BF16, name="x_bf", align_bytes=64)
+            for b in range(3):
+                tp = psum.tile([P, 2, 2, P], F32, name="tp", tag="tp", bufs=3)
+                for s in range(2):
+                    i, g = divmod(2 * b + s, GX)
+                    for u in range(2):
+                        nc.tensor.transpose(tp[:, s, u, :], x_split[n][:, i, u, 128 * g : 128 * g + 128], ident[:])
+                dst = xb[:, 1024 * b : 1024 * b + 1024].bitcast(F32).rearrange("p (s m u) -> p s m u", s=2, u=2)
+                src = tp[:].rearrange("p s u m -> p s m u")
+                if b == 1:
+                    nc.vector.tensor_copy(out=dst, in_=src)
+                else:
+                    nc.scalar.copy(out=dst, in_=src)
+            x_bf[n] = xb
+
+        def quant_x(n):
+            xc = work.tile([P, 6 * 128], U32, name="x_codes", align_bytes=64)
+            xs = work.tile([P, 6 * 128], U8, name="x_scales", align_bytes=64)
+            for b in range(3):
+                nc.vector.quantize_mx(
+                    out=xc[:, 256 * b : 256 * b + 256].bitcast(FP8),
+                    scales=xs[:, 256 * b : 256 * b + 256],
+                    in_=x_bf[n][:, 1024 * b : 1024 * b + 1024],
+                )
+            x_codes[n], x_scales[n] = xc, xs
+
+        feat_bf = {}
+        feat_codes = {}
+        feat_scales = {}
+
+        def stage1(i, h):
+            n, k = divmod(i, 2)
+            if h == 0:
+                feat_bf[i] = work.tile([P, H, 512], BF16, name="feat_bf", align_bytes=64)
+            acc = psum.tile([P, 4, P], F32, name="acc", tag="acc", bufs=3)
+            for t in range(4):
+                for g in range(GX):
+                    cols = slice(128 * (3 * k + g), 128 * (3 * k + g) + 128)
+                    nc.tensor.matmul_mx(
+                        out=acc[:, t, :],
+                        lhsT=w_codes[h][g][:, 128 * t : 128 * t + 128].bitcast(FP8),
+                        lhsT_scale=w_scales[h][g][:, 128 * t : 128 * t + 128],
+                        rhs=x_codes[n][:, cols].bitcast(FP8),
+                        rhs_scale=x_scales[n][:, cols],
+                        start=(g == 0),
+                        stop=(g == GX - 1),
+                    )
+            nc.scalar.activation(
+                out=feat_bf[i][:, h, :].rearrange("p (m t) -> p m t", t=4),
+                in_=acc[:].rearrange("p t m -> p m t"),
+                func=RELU,
+            )
+
+        def quant_feat(i):
+            fc = work.tile([P, H * P], U32, name="feat_codes", bufs=4, align_bytes=64)
+            fs = work.tile([P, H * P], U8, name="feat_scales", bufs=4, align_bytes=64)
+            nc.vector.quantize_mx(out=fc[:].bitcast(FP8), scales=fs[:], in_=feat_bf[i][:].rearrange("p h k -> p (h k)"))
+            feat_codes[i], feat_scales[i] = fc, fs
+
+        score = keep.tile([P, TILES], F32, name="score")
+        err = {}
+
+        def stage2(i):
+            n, k = divmod(i, 2)
+            if k == 0:
+                err[n] = work.tile([P, 2, C], F32, name="err", align_bytes=64)
+            res = psum.tile([P, C], F32, name="res", tag="res", bufs=2)
+            for h in range(H):
+                nc.tensor.matmul_mx(
+                    out=res[:],
+                    lhsT=feat_codes[i][:, 128 * h : 128 * h + 128].bitcast(FP8),
+                    lhsT_scale=feat_scales[i][:, 128 * h : 128 * h + 128],
+                    rhs=head_codes[:, h, :].bitcast(FP8),
+                    rhs_scale=head_scales[:, h, :],
+                    start=(h == 0),
+                    stop=(h == H - 1),
+                )
+            nc.vector.tensor_tensor(out=err[n][:, k, :], in0=res[:], in1=y_sb[i // 4][:, i % 4, :], op=SUB)
+            junk = work.tile([P, C], BF16, name="junk")
+            nc.scalar.activation(
+                out=junk[:], in_=err[n][:, k, :], func=SQUARE, scale=1.0 / C**0.5, accum_out=score[:, i : i + 1]
+            )
+            if n == PAIRS - 1:
+                nc.sync.dma_start(out=out_rows[:, i, :], in_=err[n][:, k, :])
+            elif k == 1:
+                nc.sync.dma_start(out=out_rows[:, 2 * n : 2 * n + 2, :], in_=err[n][:])
+
+        prep_w(0)
+        split_x(0)
+        turn_x(0)
+        quant_x(0)
+        prep_w(1)
+        for h in range(H):
+            nc.vector.quantize_mx(out=head_codes[:, h, :].bitcast(FP8), scales=head_scales[:, h, :], in_=head_bf[:, h, :])
+        split_x(1)
+        for n in range(PAIRS):
+            if n + 2 < PAIRS:
+                split_x(n + 2)
+            if n + 1 < PAIRS:
+                turn_x(n + 1)
+            order = [(0, 0), (1, 0), (0, 1), (1, 1)] if n == 0 else [(0, 0), (0, 1), (1, 0), (1, 1)]
+            for k, h in order:
+                stage1(2 * n + k, h)
+            if n + 1 < PAIRS:
+                quant_x(n + 1)
+            if n > 0:
+                stage2(2 * n - 2)
+                stage2(2 * n - 1)
+            quant_feat(2 * n)
+            quant_feat(2 * n + 1)
+        stage2(TILES - 2)
+        stage2(TILES - 1)
+        nc.sync.dma_start(out=out_1.rearrange("(p i) -> p i", i=TILES), in_=score[:])

@@ -13,7 +13,6 @@ U32 = mybir.dt.uint32
 U8 = mybir.dt.uint8
 FP8 = mybir.dt.float8_e4m3fn_x4
 FP4 = mybir.dt.float4_e2m1fn_x4
-COPY = mybir.ActivationFunctionType.Copy
 RELU = mybir.ActivationFunctionType.Relu
 SQUARE = mybir.ActivationFunctionType.Square
 SUB = mybir.AluOpType.subtract
@@ -24,6 +23,7 @@ GR = R // 512
 H = D // 512
 TILES = M // P
 PAIRS = TILES // 2
+FIRST = 2
 
 
 def tile_el2n_pruning_score_s12_kernel(tc, x, w, u_words, u_scales, v_words, v_scales, y, out_0, out_1):
@@ -31,8 +31,11 @@ def tile_el2n_pruning_score_s12_kernel(tc, x, w, u_words, u_scales, v_words, v_s
     with ExitStack() as ctx:
         keep = ctx.enter_context(tc.tile_pool(name="keep", bufs=1))
         work = ctx.enter_context(tc.tile_pool(name="work", bufs=3))
-        psum = ctx.enter_context(tc.psum_pool(name="psum", bufs=3))
+        psum = ctx.enter_context(tc.psum_pool(name="psum", bufs=5))
+        ctx.enter_context(tc.manual_schedule())
 
+        ident = keep.tile([P, P], F32, name="ident")
+        make_identity(nc, ident[:])
         u_plane = keep.tile([P, GR, D], U8, name="u_plane", align_bytes=64)
         v_plane = keep.tile([P, GR, C], U8, name="v_plane", align_bytes=64)
         nc.vector.memset(v_plane[:].bitcast(I32), 0)
@@ -40,19 +43,14 @@ def tile_el2n_pruning_score_s12_kernel(tc, x, w, u_words, u_scales, v_words, v_s
         warm = keep.tile([P, 1], F32, name="warm")
         nc.vector.memset(warm[:], 0.0)
         warm2 = keep.tile([P, 1], F32, name="warm2")
-        nc.scalar.activation(out=warm2[:], in_=warm[:], func=RELU)
 
         u_raw = keep.tile([P, GR, 2 * D], U8, name="u_raw", align_bytes=64)
         v_raw = keep.tile([P, GR, 2 * C], U8, name="v_raw", align_bytes=64)
-        nc.sync.dma_start(out=u_raw[:].bitcast(I32), in_=u_words.bitcast(I32).rearrange("g p n -> p g n"))
-        nc.sync.dma_start(out=v_raw[:].bitcast(I32), in_=v_words.bitcast(I32).rearrange("g p n -> p g n"))
         us = u_scales.bitcast(I32).rearrange("g q n -> q g n")
         vs = v_scales.bitcast(I32).rearrange("g q n -> q g n")
-        for q in range(4):
-            nc.scalar.dma_start(out=u_plane[32 * q : 32 * q + 4].bitcast(I32), in_=us[4 * q : 4 * q + 4])
-            nc.gpsimd.dma_start(out=v_plane[32 * q : 32 * q + 4].bitcast(I32), in_=vs[4 * q : 4 * q + 4])
-        ident = keep.tile([P, P], F32, name="ident")
-        make_identity(nc, ident[:])
+        def load_scales(queue, plane, rows, qs):
+            for q in qs:
+                queue.dma_start(out=plane[32 * q : 32 * q + 4].bitcast(I32), in_=rows[4 * q : 4 * q + 4])
 
         x_rows = x.rearrange("(p i) k -> p i k", i=TILES)
         y_rows = y.rearrange("(p i) c -> p i c", i=TILES)
@@ -73,10 +71,16 @@ def tile_el2n_pruning_score_s12_kernel(tc, x, w, u_words, u_scales, v_words, v_s
         def load_y(n):
             nc.sync.dma_start(out=y_sb[n][:], in_=y_rows[:, 4 * n : 4 * n + 4, :])
 
+        load_scales(nc.gpsimd, v_plane, vs, (2, 3))
+        load_scales(nc.scalar, v_plane, vs, (0, 1))
+        load_scales(nc.scalar, u_plane, us, (0, 1, 2, 3))
+        nc.sync.dma_start(out=u_raw[:].bitcast(I32), in_=u_words.bitcast(I32).rearrange("g p n -> p g n"))
         load_x(0)
+        nc.sync.dma_start(out=v_raw[:].bitcast(I32), in_=v_words.bitcast(I32).rearrange("g p n -> p g n"))
+        nc.scalar.activation(out=warm2[:], in_=warm[:], func=RELU)
         load_w(0)
-        load_w(1)
         load_x(1)
+        load_w(1)
         load_x(2)
         load_y(0)
         load_x(3)
@@ -90,56 +94,74 @@ def tile_el2n_pruning_score_s12_kernel(tc, x, w, u_words, u_scales, v_words, v_s
 
         u_codes = keep.tile([P, GR, 2 * D], U8, name="u_codes", align_bytes=64)
         u_perm = keep.tile([P, GR, D], U8, name="u_perm", align_bytes=64)
-        for g in range(GR):
-            nc.vector.tensor_copy(
-                out=u_codes[:, g, :].bitcast(I32).rearrange("p (t q b) -> p t q b", t=4, b=4),
-                in_=u_raw[:, g, :].bitcast(I32).rearrange("p (q t b) -> p t q b", t=4, b=4),
-            )
-        for g in range(GR):
-            nc.vector.tensor_copy(
-                out=u_perm[:, g, :].bitcast(I32).rearrange("p (t q b) -> p t q b", t=4, b=2),
-                in_=u_plane[:, g, :].bitcast(I32).rearrange("p (q t b) -> p t q b", t=4, b=2),
-            )
+
+        def order_u():
+            for g in range(GR):
+                nc.vector.tensor_copy(
+                    out=u_codes[:, g, :].bitcast(I32).rearrange("p (t q b) -> p t q b", t=4, b=2),
+                    in_=u_raw[:, g, :].bitcast(I32).rearrange("p (q t b) -> p t q b", t=4, b=2),
+                )
+            for g in range(GR):
+                nc.vector.tensor_copy(
+                    out=u_perm[:, g, :].bitcast(I32).rearrange("p (t q) -> p t q", t=4),
+                    in_=u_plane[:, g, :].bitcast(I32).rearrange("p (q t) -> p t q", t=4),
+                )
 
         head_bf = keep.tile([P, H, 4 * C], BF16, name="head_bf", align_bytes=64)
         head_codes = keep.tile([P, H, C], U32, name="head_codes", align_bytes=64)
         head_scales = keep.tile([P, H, C], U8, name="head_scales", align_bytes=64)
-        for h in range(H):
-            for cc in range(4):
-                acc = psum.tile([P, 4, P], F32, name="acc", tag="acc", bufs=3)
-                for t in range(4):
-                    col = 256 * t + 128 * h
-                    for g in range(GR):
-                        nc.tensor.matmul_mx(
-                            out=acc[:, t, :],
-                            lhsT=u_codes[:, g, 2 * col : 2 * col + 256].bitcast(FP4),
-                            lhsT_scale=u_perm[:, g, col : col + 128],
-                            rhs=v_raw[:, g, 256 * cc : 256 * cc + 256].bitcast(FP4),
-                            rhs_scale=v_plane[:, g, 128 * cc : 128 * cc + 128],
-                            start=(g == 0),
-                            stop=(g == GR - 1),
-                        )
-                dst = head_bf[:, h, 512 * cc : 512 * cc + 512].rearrange("p (c t) -> p c t", t=4)
-                src = acc[:].rearrange("p t c -> p c t")
-                if cc == 3:
-                    nc.vector.tensor_copy(out=dst, in_=src)
-                else:
-                    nc.scalar.copy(out=dst, in_=src)
+        banks = {}
+
+        def head(n):
+            h, cc = divmod(n, 4)
+            acc = psum.tile([P, 4, P], F32, name="acc", tag="acc", bufs=5)
+            for t in range(4):
+                col = 256 * t + 128 * h
+                for g in range(GR):
+                    nc.tensor.matmul_mx(
+                        out=acc[:, t, :],
+                        lhsT=u_codes[:, g, 2 * col : 2 * col + 256].bitcast(FP4),
+                        lhsT_scale=u_perm[:, g, col : col + 128],
+                        rhs=v_raw[:, g, 256 * cc : 256 * cc + 256].bitcast(FP4),
+                        rhs_scale=v_plane[:, g, 128 * cc : 128 * cc + 128],
+                        start=(g == 0),
+                        stop=(g == GR - 1),
+                    )
+            banks["head", n] = acc
+
+        def copy_out(engine, dst, src):
+            if engine == "S":
+                nc.scalar.copy(out=dst, in_=src)
+            else:
+                nc.vector.tensor_copy(out=dst, in_=src)
+
+        def head_out(n, engine="S"):
+            h, cc = divmod(n, 4)
+            dst = head_bf[:, h, 512 * cc : 512 * cc + 512].rearrange("p (c t) -> p c t", t=4)
+            copy_out(engine, dst, banks["head", n][:].rearrange("p t c -> p c t"))
+
+        def quant_head():
+            for h in range(H):
+                nc.vector.quantize_mx(
+                    out=head_codes[:, h, :].bitcast(FP8), scales=head_scales[:, h, :], in_=head_bf[:, h, :]
+                )
 
         w_bf = [[keep.tile([P, 2048], BF16, name=f"w_bf{h}{g}", align_bytes=64) for g in range(GX)] for h in range(H)]
         w_codes = [[keep.tile([P, 512], U32, name=f"w_codes{h}{g}", align_bytes=64) for g in range(GX)] for h in range(H)]
         w_scales = [[keep.tile([P, 512], U8, name=f"w_scales{h}{g}", align_bytes=64) for g in range(GX)] for h in range(H)]
 
-        def prep_w(h):
-            for g in range(GX):
-                src = w_raw[h][g][:].rearrange("p j (q t r) -> p t q r j", t=4, r=8)
-                dst = w_bf[h][g][:].rearrange("p (t q r j) -> p t q r j", t=4, r=8, j=4)
-                for t in range(4):
-                    if t == 3:
-                        nc.scalar.copy(out=dst[:, t], in_=src[:, t])
-                    else:
-                        nc.vector.tensor_copy(out=dst[:, t], in_=src[:, t])
-                nc.vector.quantize_mx(out=w_codes[h][g][:].bitcast(FP8), scales=w_scales[h][g][:], in_=w_bf[h][g][:])
+        def copy_w(h, g, half):
+            src = w_raw[h][g][:].rearrange("p j (q t b) -> p t q j b", t=4, b=4)
+            dst = w_bf[h][g][:].rearrange("p (t q b j) -> p t q j b", t=4, b=4, j=4)
+            for t in (2 * half, 2 * half + 1):
+                copy_out("S" if t == 3 else "V", dst[:, t], src[:, t])
+
+        def quant_w(h, g, half):
+            nc.vector.quantize_mx(
+                out=w_codes[h][g][:, 256 * half : 256 * half + 256].bitcast(FP8),
+                scales=w_scales[h][g][:, 256 * half : 256 * half + 256],
+                in_=w_bf[h][g][:, 1024 * half : 1024 * half + 1024],
+            )
 
         x_split = {}
         x_bf = {}
@@ -152,19 +174,24 @@ def tile_el2n_pruning_score_s12_kernel(tc, x, w, u_words, u_scales, v_words, v_s
             x_split[n] = xs
 
         def turn_x(n):
-            xb = work.tile([P, 6 * 512], BF16, name="x_bf", align_bytes=64)
+            words = x_raw[n][:].bitcast(F32)
             for b in range(3):
                 tp = psum.tile([P, 2, 2, P], F32, name="tp", tag="tp", bufs=3)
                 for s in range(2):
                     i, g = divmod(2 * b + s, GX)
                     for u in range(2):
-                        nc.tensor.transpose(tp[:, s, u, :], x_split[n][:, i, u, 128 * g : 128 * g + 128], ident[:])
+                        if n < FIRST:
+                            src = words[:, i, 256 * g + u : 256 * g + 256 : 2]
+                        else:
+                            src = x_split[n][:, i, u, 128 * g : 128 * g + 128]
+                        nc.tensor.transpose(tp[:, s, u, :], src, ident[:])
+                banks["x", n, b] = tp
+
+        def x_out(n, engines):
+            xb = work.tile([P, 6 * 512], BF16, name="x_bf", align_bytes=64)
+            for b in range(3):
                 dst = xb[:, 1024 * b : 1024 * b + 1024].bitcast(F32).rearrange("p (s m u) -> p s m u", s=2, u=2)
-                src = tp[:].rearrange("p s u m -> p s m u")
-                if b == 1:
-                    nc.vector.tensor_copy(out=dst, in_=src)
-                else:
-                    nc.scalar.copy(out=dst, in_=src)
+                copy_out(engines[b], dst, banks["x", n, b][:].rearrange("p s u m -> p s m u"))
             x_bf[n] = xb
 
         def quant_x(n):
@@ -182,12 +209,12 @@ def tile_el2n_pruning_score_s12_kernel(tc, x, w, u_words, u_scales, v_words, v_s
         feat_codes = {}
         feat_scales = {}
 
-        def stage1(i, h):
+        def stage1(i, h, ts):
             n, k = divmod(i, 2)
-            if h == 0:
-                feat_bf[i] = work.tile([P, H, 512], BF16, name="feat_bf", align_bytes=64)
-            acc = psum.tile([P, 4, P], F32, name="acc", tag="acc", bufs=3)
-            for t in range(4):
+            if 0 in ts:
+                banks["feat", i, h] = psum.tile([P, 4, P], F32, name="acc", tag="acc", bufs=5)
+            acc = banks["feat", i, h]
+            for t in ts:
                 for g in range(GX):
                     cols = slice(128 * (3 * k + g), 128 * (3 * k + g) + 128)
                     nc.tensor.matmul_mx(
@@ -199,15 +226,19 @@ def tile_el2n_pruning_score_s12_kernel(tc, x, w, u_words, u_scales, v_words, v_s
                         start=(g == 0),
                         stop=(g == GX - 1),
                     )
+
+        def feat_out(i, h):
+            if h == 0:
+                feat_bf[i] = work.tile([P, H, 512], BF16, name="feat_bf", bufs=5, align_bytes=64)
             nc.scalar.activation(
                 out=feat_bf[i][:, h, :].rearrange("p (m t) -> p m t", t=4),
-                in_=acc[:].rearrange("p t m -> p m t"),
+                in_=banks["feat", i, h][:].rearrange("p t m -> p m t"),
                 func=RELU,
             )
 
         def quant_feat(i):
-            fc = work.tile([P, H * P], U32, name="feat_codes", bufs=4, align_bytes=64)
-            fs = work.tile([P, H * P], U8, name="feat_scales", bufs=4, align_bytes=64)
+            fc = work.tile([P, H * P], U32, name="feat_codes", bufs=8, align_bytes=64)
+            fs = work.tile([P, H * P], U8, name="feat_scales", bufs=8, align_bytes=64)
             nc.vector.quantize_mx(out=fc[:].bitcast(FP8), scales=fs[:], in_=feat_bf[i][:].rearrange("p h k -> p (h k)"))
             feat_codes[i], feat_scales[i] = fc, fs
 
@@ -218,7 +249,7 @@ def tile_el2n_pruning_score_s12_kernel(tc, x, w, u_words, u_scales, v_words, v_s
             n, k = divmod(i, 2)
             if k == 0:
                 err[n] = work.tile([P, 2, C], F32, name="err", align_bytes=64)
-            res = psum.tile([P, C], F32, name="res", tag="res", bufs=2)
+            res = psum.tile([P, C], F32, name="res", tag="acc", bufs=5)
             for h in range(H):
                 nc.tensor.matmul_mx(
                     out=res[:],
@@ -230,7 +261,7 @@ def tile_el2n_pruning_score_s12_kernel(tc, x, w, u_words, u_scales, v_words, v_s
                     stop=(h == H - 1),
                 )
             nc.vector.tensor_tensor(out=err[n][:, k, :], in0=res[:], in1=y_sb[i // 4][:, i % 4, :], op=SUB)
-            junk = work.tile([P, C], BF16, name="junk")
+            junk = work.tile([P, C], BF16, name="junk", bufs=2)
             nc.scalar.activation(
                 out=junk[:], in_=err[n][:, k, :], func=SQUARE, scale=1.0 / C**0.5, accum_out=score[:, i : i + 1]
             )
@@ -239,29 +270,82 @@ def tile_el2n_pruning_score_s12_kernel(tc, x, w, u_words, u_scales, v_words, v_s
             elif k == 1:
                 nc.sync.dma_start(out=out_rows[:, 2 * n : 2 * n + 2, :], in_=err[n][:])
 
-        prep_w(0)
-        split_x(0)
+        heads = [0]
+
+        def head_step():
+            n = heads[0]
+            if n < 8:
+                head_out(n)
+                if n + 5 < 8:
+                    head(n + 5)
+                heads[0] = n + 1
+
+        order_u()
         turn_x(0)
+        x_out(0, "SSS")
         quant_x(0)
-        prep_w(1)
-        for h in range(H):
-            nc.vector.quantize_mx(out=head_codes[:, h, :].bitcast(FP8), scales=head_scales[:, h, :], in_=head_bf[:, h, :])
-        split_x(1)
-        for n in range(PAIRS):
-            if n + 2 < PAIRS:
-                split_x(n + 2)
+        for n in range(5):
+            head(n)
+        for half in range(2):
+            for g in range(GX):
+                copy_w(0, g, half)
+                if g > 0:
+                    quant_w(0, g - 1, half)
+                head_step()
+                if half == 0 and g == 0:
+                    turn_x(1)
+            quant_w(0, 2, half)
+            if half == 0:
+                x_out(1, "SVV")
+                quant_x(1)
+            else:
+                head_step()
+                head_step()
+            for i in range(4):
+                stage1(i, 0, (2 * half, 2 * half + 1))
+        for i in range(4):
+            feat_out(i, 0)
+        for half in range(2):
+            for g in range(GX):
+                copy_w(1, g, half)
+                if g > 0:
+                    quant_w(1, g - 1, half)
+                if half == 0 and g == 0:
+                    split_x(2)
+            quant_w(1, 2, half)
+            if half == 0:
+                turn_x(2)
+                x_out(2, "SVS")
+            for i in range(4):
+                stage1(i, 1, (2 * half, 2 * half + 1))
+            if half == 0:
+                quant_x(2)
+        quant_head()
+        for i in range(4):
+            feat_out(i, 1)
+        split_x(3)
+        for i in range(4):
+            quant_feat(i)
+        for n in range(2, PAIRS):
             if n + 1 < PAIRS:
                 turn_x(n + 1)
-            order = [(0, 0), (1, 0), (0, 1), (1, 1)] if n == 0 else [(0, 0), (0, 1), (1, 0), (1, 1)]
-            for k, h in order:
-                stage1(2 * n + k, h)
+                x_out(n + 1, "SVS")
+            for h in range(H):
+                stage1(2 * n, h, range(4))
+                feat_out(2 * n, h)
             if n + 1 < PAIRS:
                 quant_x(n + 1)
-            if n > 0:
-                stage2(2 * n - 2)
-                stage2(2 * n - 1)
+            if n + 2 < PAIRS:
+                split_x(n + 2)
+            stage1(2 * n + 1, 0, range(4))
+            feat_out(2 * n + 1, 0)
             quant_feat(2 * n)
-            quant_feat(2 * n + 1)
+            stage1(2 * n + 1, 1, range(4))
+            feat_out(2 * n + 1, 1)
+            for i in range(0 if n == 2 else 2 * n - 2, 2 * n):
+                stage2(i)
+                if i == 2 * n - 2:
+                    quant_feat(2 * n + 1)
         stage2(TILES - 2)
         stage2(TILES - 1)
         nc.sync.dma_start(out=out_1.rearrange("(p i) -> p i", i=TILES), in_=score[:])

@@ -23,7 +23,7 @@ GR = R // 512
 H = D // 512
 TILES = M // P
 PAIRS = TILES // 2
-FIRST = 2
+FIRST = 3
 
 
 def tile_el2n_pruning_score_s12_kernel(tc, x, w, u_words, u_scales, v_words, v_scales, y, out_0, out_1):
@@ -36,6 +36,8 @@ def tile_el2n_pruning_score_s12_kernel(tc, x, w, u_words, u_scales, v_words, v_s
 
         ident = keep.tile([P, P], F32, name="ident")
         make_identity(nc, ident[:])
+        zeros = keep.tile([P, C], BF16, name="zeros", align_bytes=64)
+        nc.gpsimd.memset(zeros[:], 0.0)
         u_plane = keep.tile([P, GR, D], U8, name="u_plane", align_bytes=64)
         v_plane = keep.tile([P, GR, C], U8, name="v_plane", align_bytes=64)
         nc.vector.memset(v_plane[:].bitcast(I32), 0)
@@ -61,9 +63,8 @@ def tile_el2n_pruning_score_s12_kernel(tc, x, w, u_words, u_scales, v_words, v_s
         y_sb = [keep.tile([P, 4, C], BF16, name=f"y_sb{n}", align_bytes=64) for n in range(TILES // 4)]
         w_raw = [[keep.tile([P, 4, 512], BF16, name=f"w_raw{h}{g}", align_bytes=64) for g in range(GX)] for h in range(H)]
 
-        def load_w(h):
-            for g in range(GX):
-                nc.sync.dma_start(out=w_raw[h][g][:], in_=w_rows[g][:, :, 512 * h : 512 * h + 512])
+        def load_w(h, g):
+            nc.sync.dma_start(out=w_raw[h][g][:], in_=w_rows[g][:, :, 512 * h : 512 * h + 512])
 
         def load_x(n):
             nc.sync.dma_start(out=x_raw[n][:], in_=x_rows[:, 2 * n : 2 * n + 2, :])
@@ -74,14 +75,18 @@ def tile_el2n_pruning_score_s12_kernel(tc, x, w, u_words, u_scales, v_words, v_s
         load_scales(nc.gpsimd, v_plane, vs, (2, 3))
         load_scales(nc.scalar, v_plane, vs, (0, 1))
         load_scales(nc.scalar, u_plane, us, (0, 1, 2, 3))
+        nc.scalar.activation(out=warm2[:], in_=warm[:], func=RELU)
+        load_w(0, 0)
         nc.sync.dma_start(out=u_raw[:].bitcast(I32), in_=u_words.bitcast(I32).rearrange("g p n -> p g n"))
         load_x(0)
         nc.sync.dma_start(out=v_raw[:].bitcast(I32), in_=v_words.bitcast(I32).rearrange("g p n -> p g n"))
-        nc.scalar.activation(out=warm2[:], in_=warm[:], func=RELU)
-        load_w(0)
+        load_w(0, 2)
+        load_w(0, 1)
         load_x(1)
-        load_w(1)
+        load_w(1, 2)
         load_x(2)
+        load_w(1, 0)
+        load_w(1, 1)
         load_y(0)
         load_x(3)
         load_x(4)
@@ -95,17 +100,17 @@ def tile_el2n_pruning_score_s12_kernel(tc, x, w, u_words, u_scales, v_words, v_s
         u_codes = keep.tile([P, GR, 2 * D], U8, name="u_codes", align_bytes=64)
         u_perm = keep.tile([P, GR, D], U8, name="u_perm", align_bytes=64)
 
-        def order_u():
-            for g in range(GR):
-                nc.vector.tensor_copy(
-                    out=u_codes[:, g, :].bitcast(I32).rearrange("p (t q b) -> p t q b", t=4, b=2),
-                    in_=u_raw[:, g, :].bitcast(I32).rearrange("p (q t b) -> p t q b", t=4, b=2),
-                )
-            for g in range(GR):
-                nc.vector.tensor_copy(
-                    out=u_perm[:, g, :].bitcast(I32).rearrange("p (t q) -> p t q", t=4),
-                    in_=u_plane[:, g, :].bitcast(I32).rearrange("p (q t) -> p t q", t=4),
-                )
+        def order_codes(g):
+            nc.vector.tensor_copy(
+                out=u_codes[:, g, :].bitcast(I32).rearrange("p (t q b) -> p t q b", t=4, b=2),
+                in_=u_raw[:, g, :].bitcast(I32).rearrange("p (q t b) -> p t q b", t=4, b=2),
+            )
+
+        def order_scales(g):
+            nc.vector.tensor_copy(
+                out=u_perm[:, g, :].bitcast(I32).rearrange("p (t q) -> p t q", t=4),
+                in_=u_plane[:, g, :].bitcast(I32).rearrange("p (q t) -> p t q", t=4),
+            )
 
         head_bf = keep.tile([P, H, 4 * C], BF16, name="head_bf", align_bytes=64)
         head_codes = keep.tile([P, H, C], U32, name="head_codes", align_bytes=64)
@@ -140,21 +145,24 @@ def tile_el2n_pruning_score_s12_kernel(tc, x, w, u_words, u_scales, v_words, v_s
             dst = head_bf[:, h, 512 * cc : 512 * cc + 512].rearrange("p (c t) -> p c t", t=4)
             copy_out(engine, dst, banks["head", n][:].rearrange("p t c -> p c t"))
 
-        def quant_head():
-            for h in range(H):
-                nc.vector.quantize_mx(
-                    out=head_codes[:, h, :].bitcast(FP8), scales=head_scales[:, h, :], in_=head_bf[:, h, :]
-                )
+        def quant_head(h):
+            nc.vector.quantize_mx(
+                out=head_codes[:, h, :].bitcast(FP8), scales=head_scales[:, h, :], in_=head_bf[:, h, :]
+            )
 
         w_bf = [[keep.tile([P, 2048], BF16, name=f"w_bf{h}{g}", align_bytes=64) for g in range(GX)] for h in range(H)]
         w_codes = [[keep.tile([P, 512], U32, name=f"w_codes{h}{g}", align_bytes=64) for g in range(GX)] for h in range(H)]
         w_scales = [[keep.tile([P, 512], U8, name=f"w_scales{h}{g}", align_bytes=64) for g in range(GX)] for h in range(H)]
 
-        def copy_w(h, g, half):
+        def copy_w(h, g, half, engines):
             src = w_raw[h][g][:].rearrange("p j (q t b) -> p t q j b", t=4, b=4)
             dst = w_bf[h][g][:].rearrange("p (t q b j) -> p t q j b", t=4, b=4, j=4)
-            for t in (2 * half, 2 * half + 1):
-                copy_out("S" if t == 3 else "V", dst[:, t], src[:, t])
+            t = 2 * half
+            if engines == "VV":
+                nc.vector.tensor_copy(out=dst[:, t : t + 2], in_=src[:, t : t + 2])
+            else:
+                copy_out(engines[0], dst[:, t], src[:, t])
+                copy_out(engines[1], dst[:, t + 1], src[:, t + 1])
 
         def quant_w(h, g, half):
             nc.vector.quantize_mx(
@@ -173,179 +181,428 @@ def tile_el2n_pruning_score_s12_kernel(tc, x, w, u_words, u_scales, v_words, v_s
             nc.vector.tensor_copy(out=xs[:], in_=x_raw[n][:].bitcast(F32).rearrange("p i (w u) -> p i u w", u=2))
             x_split[n] = xs
 
-        def turn_x(n):
+        def turn_x(n, g):
             words = x_raw[n][:].bitcast(F32)
-            for b in range(3):
-                tp = psum.tile([P, 2, 2, P], F32, name="tp", tag="tp", bufs=3)
-                for s in range(2):
-                    i, g = divmod(2 * b + s, GX)
-                    for u in range(2):
-                        if n < FIRST:
-                            src = words[:, i, 256 * g + u : 256 * g + 256 : 2]
-                        else:
-                            src = x_split[n][:, i, u, 128 * g : 128 * g + 128]
-                        nc.tensor.transpose(tp[:, s, u, :], src, ident[:])
-                banks["x", n, b] = tp
+            tp = psum.tile([P, 2, 2, P], F32, name="tp", tag="tp", bufs=3)
+            for i in range(2):
+                for u in range(2):
+                    if n < FIRST:
+                        src = words[:, i, 256 * g + u : 256 * g + 256 : 2]
+                    else:
+                        src = x_split[n][:, i, u, 128 * g : 128 * g + 128]
+                    nc.tensor.transpose(tp[:, i, u, :], src, ident[:])
+            banks["x", n, g] = tp
 
-        def x_out(n, engines):
-            xb = work.tile([P, 6 * 512], BF16, name="x_bf", align_bytes=64)
-            for b in range(3):
-                dst = xb[:, 1024 * b : 1024 * b + 1024].bitcast(F32).rearrange("p (s m u) -> p s m u", s=2, u=2)
-                copy_out(engines[b], dst, banks["x", n, b][:].rearrange("p s u m -> p s m u"))
-            x_bf[n] = xb
+        def x_out(n, g, engine):
+            if n not in x_bf:
+                x_bf[n] = work.tile([P, 6 * 512], BF16, name="x_bf", align_bytes=64)
+            dst = x_bf[n][:, 1024 * g : 1024 * g + 1024].bitcast(F32).rearrange("p (i m u) -> p i m u", i=2, u=2)
+            copy_out(engine, dst, banks["x", n, g][:].rearrange("p i u m -> p i m u"))
 
-        def quant_x(n):
-            xc = work.tile([P, 6 * 128], U32, name="x_codes", align_bytes=64)
-            xs = work.tile([P, 6 * 128], U8, name="x_scales", align_bytes=64)
-            for b in range(3):
-                nc.vector.quantize_mx(
-                    out=xc[:, 256 * b : 256 * b + 256].bitcast(FP8),
-                    scales=xs[:, 256 * b : 256 * b + 256],
-                    in_=x_bf[n][:, 1024 * b : 1024 * b + 1024],
-                )
-            x_codes[n], x_scales[n] = xc, xs
+        def quant_x(n, g):
+            if n not in x_codes:
+                x_codes[n] = work.tile([P, 6 * 128], U32, name="x_codes", align_bytes=64)
+                x_scales[n] = work.tile([P, 6 * 128], U8, name="x_scales", align_bytes=64)
+            nc.vector.quantize_mx(
+                out=x_codes[n][:, 256 * g : 256 * g + 256].bitcast(FP8),
+                scales=x_scales[n][:, 256 * g : 256 * g + 256],
+                in_=x_bf[n][:, 1024 * g : 1024 * g + 1024],
+            )
 
         feat_bf = {}
         feat_codes = {}
         feat_scales = {}
 
-        def stage1(i, h, ts):
+        def open_feat(n):
+            if n not in feat_bf:
+                feat_bf[n] = work.tile([P, H, 1024], BF16, name="feat_bf", bufs=3, align_bytes=64)
+
+        def passes(acc, n, h, t, cols):
+            for g in range(GX):
+                at = slice(256 * g + cols.start, 256 * g + cols.stop)
+                nc.tensor.matmul_mx(
+                    out=acc,
+                    lhsT=w_codes[h][g][:, 128 * t : 128 * t + 128].bitcast(FP8),
+                    lhsT_scale=w_scales[h][g][:, 128 * t : 128 * t + 128],
+                    rhs=x_codes[n][:, at].bitcast(FP8),
+                    rhs_scale=x_scales[n][:, at],
+                    start=(g == 0),
+                    stop=(g == GX - 1),
+                )
+
+        def narrow(i, h, half):
             n, k = divmod(i, 2)
-            if 0 in ts:
+            if ("feat", i, h) not in banks:
                 banks["feat", i, h] = psum.tile([P, 4, P], F32, name="acc", tag="acc", bufs=5)
-            acc = banks["feat", i, h]
-            for t in ts:
-                for g in range(GX):
-                    cols = slice(128 * (3 * k + g), 128 * (3 * k + g) + 128)
-                    nc.tensor.matmul_mx(
-                        out=acc[:, t, :],
-                        lhsT=w_codes[h][g][:, 128 * t : 128 * t + 128].bitcast(FP8),
-                        lhsT_scale=w_scales[h][g][:, 128 * t : 128 * t + 128],
-                        rhs=x_codes[n][:, cols].bitcast(FP8),
-                        rhs_scale=x_scales[n][:, cols],
-                        start=(g == 0),
-                        stop=(g == GX - 1),
-                    )
+            for t in (2 * half, 2 * half + 1):
+                passes(banks["feat", i, h][:, t, :], n, h, t, slice(128 * k, 128 * k + 128))
 
-        def feat_out(i, h):
-            if h == 0:
-                feat_bf[i] = work.tile([P, H, 512], BF16, name="feat_bf", bufs=5, align_bytes=64)
-            nc.scalar.activation(
-                out=feat_bf[i][:, h, :].rearrange("p (m t) -> p m t", t=4),
-                in_=banks["feat", i, h][:].rearrange("p t m -> p m t"),
-                func=RELU,
+        def relu_out(engine, dst, src):
+            if engine == "S":
+                nc.scalar.activation(out=dst, in_=src, func=RELU)
+            else:
+                nc.vector.tensor_scalar_max(out=dst, in0=src, scalar1=0.0)
+
+        def narrow_out(i, h, engine):
+            n, k = divmod(i, 2)
+            open_feat(n)
+            dst = feat_bf[n][:, h, 512 * k : 512 * k + 512].rearrange("p (m t) -> p m t", t=4)
+            src = banks["feat", i, h][:].rearrange("p t m -> p m t")
+            if engine == "B":
+                relu_out("S", dst[:, 0:64], src[:, 0:64])
+                relu_out("V", dst[:, 64:128], src[:, 64:128])
+            else:
+                relu_out(engine, dst, src)
+
+        def wide(n, h, half):
+            acc = psum.tile([P, 2, 256], F32, name="acc", tag="acc", bufs=5)
+            for tt in range(2):
+                passes(acc[:, tt, :], n, h, 2 * half + tt, slice(0, 256))
+            banks["wide", n, h, half] = acc
+
+        def wide_out(n, h, half, engine):
+            open_feat(n)
+            dst = feat_bf[n][:, h, :].rearrange("p (m t) -> p m t", t=4)[:, :, 2 * half : 2 * half + 2]
+            relu_out(engine, dst, banks["wide", n, h, half][:].rearrange("p t m -> p m t"))
+
+        def quant_feat(n, h, k=None):
+            if n not in feat_codes:
+                feat_codes[n] = work.tile([P, H, 256], U32, name="feat_codes", bufs=3, align_bytes=64)
+                feat_scales[n] = work.tile([P, H, 256], U8, name="feat_scales", bufs=3, align_bytes=64)
+            rows = slice(0, 256) if k is None else slice(128 * k, 128 * k + 128)
+            nc.vector.quantize_mx(
+                out=feat_codes[n][:, h, rows].bitcast(FP8),
+                scales=feat_scales[n][:, h, rows],
+                in_=feat_bf[n][:, h, 4 * rows.start : 4 * rows.stop],
             )
-
-        def quant_feat(i):
-            fc = work.tile([P, H * P], U32, name="feat_codes", bufs=8, align_bytes=64)
-            fs = work.tile([P, H * P], U8, name="feat_scales", bufs=8, align_bytes=64)
-            nc.vector.quantize_mx(out=fc[:].bitcast(FP8), scales=fs[:], in_=feat_bf[i][:].rearrange("p h k -> p (h k)"))
-            feat_codes[i], feat_scales[i] = fc, fs
 
         score = keep.tile([P, TILES], F32, name="score")
         err = {}
 
-        def stage2(i):
+        def multiply(i, h):
             n, k = divmod(i, 2)
-            if k == 0:
+            if h == 0:
+                banks["res", i] = psum.tile([P, C], F32, name="res", tag="acc", bufs=5)
+            nc.tensor.matmul_mx(
+                out=banks["res", i][:],
+                lhsT=feat_codes[n][:, h, 128 * k : 128 * k + 128].bitcast(FP8),
+                lhsT_scale=feat_scales[n][:, h, 128 * k : 128 * k + 128],
+                rhs=head_codes[:, h, :].bitcast(FP8),
+                rhs_scale=head_scales[:, h, :],
+                start=(h == 0),
+                stop=(h == H - 1),
+            )
+
+        def subtract(i):
+            n, k = divmod(i, 2)
+            if n not in err:
                 err[n] = work.tile([P, 2, C], F32, name="err", align_bytes=64)
-            res = psum.tile([P, C], F32, name="res", tag="acc", bufs=5)
-            for h in range(H):
-                nc.tensor.matmul_mx(
-                    out=res[:],
-                    lhsT=feat_codes[i][:, 128 * h : 128 * h + 128].bitcast(FP8),
-                    lhsT_scale=feat_scales[i][:, 128 * h : 128 * h + 128],
-                    rhs=head_codes[:, h, :].bitcast(FP8),
-                    rhs_scale=head_scales[:, h, :],
-                    start=(h == 0),
-                    stop=(h == H - 1),
-                )
-            nc.vector.tensor_tensor(out=err[n][:, k, :], in0=res[:], in1=y_sb[i // 4][:, i % 4, :], op=SUB)
+            nc.vector.tensor_tensor(out=err[n][:, k, :], in0=banks["res", i][:], in1=y_sb[i // 4][:, i % 4, :], op=SUB)
+
+        def square(i):
+            n, k = divmod(i, 2)
             junk = work.tile([P, C], BF16, name="junk", bufs=2)
             nc.scalar.activation(
                 out=junk[:], in_=err[n][:, k, :], func=SQUARE, scale=1.0 / C**0.5, accum_out=score[:, i : i + 1]
             )
-            if n == PAIRS - 1:
-                nc.sync.dma_start(out=out_rows[:, i, :], in_=err[n][:, k, :])
-            elif k == 1:
+
+        def store(n, k=None):
+            if k is None:
                 nc.sync.dma_start(out=out_rows[:, 2 * n : 2 * n + 2, :], in_=err[n][:])
-
-        heads = [0]
-
-        def head_step():
-            n = heads[0]
-            if n < 8:
-                head_out(n)
-                if n + 5 < 8:
-                    head(n + 5)
-                heads[0] = n + 1
-
-        order_u()
-        turn_x(0)
-        x_out(0, "SSS")
-        quant_x(0)
-        for n in range(5):
-            head(n)
-        for half in range(2):
-            for g in range(GX):
-                copy_w(0, g, half)
-                if g > 0:
-                    quant_w(0, g - 1, half)
-                head_step()
-                if half == 0 and g == 0:
-                    turn_x(1)
-            quant_w(0, 2, half)
-            if half == 0:
-                x_out(1, "SVV")
-                quant_x(1)
             else:
-                head_step()
-                head_step()
-            for i in range(4):
-                stage1(i, 0, (2 * half, 2 * half + 1))
-        for i in range(4):
-            feat_out(i, 0)
-        for half in range(2):
-            for g in range(GX):
-                copy_w(1, g, half)
-                if g > 0:
-                    quant_w(1, g - 1, half)
-                if half == 0 and g == 0:
-                    split_x(2)
-            quant_w(1, 2, half)
-            if half == 0:
-                turn_x(2)
-                x_out(2, "SVS")
-            for i in range(4):
-                stage1(i, 1, (2 * half, 2 * half + 1))
-            if half == 0:
-                quant_x(2)
-        quant_head()
-        for i in range(4):
-            feat_out(i, 1)
+                nc.sync.dma_start(out=out_rows[:, 2 * n + k, :], in_=err[n][:, k, :])
+
+        for n in range(8):
+            dummy = psum.tile([P, C], F32, name="dummy", tag="tp", bufs=3)
+            nc.tensor.matmul(dummy[:], lhsT=zeros[:, 0:128], rhs=zeros[:], start=True, stop=True)
+        copy_w(0, 0, 0, "SS")
+        order_codes(1)
+        turn_x(0, 2)
+        order_codes(0)
+        order_scales(0)
+        copy_w(0, 0, 1, "VS")
+        x_out(0, 2, "S")
+        order_scales(1)
+        quant_w(0, 0, 0)
+        turn_x(0, 1)
+        head(0)
+        head(3)
+        x_out(0, 1, "S")
+        head_out(0, "V")
+        head(1)
+        copy_w(0, 2, 1, "VS")
+        head(4)
+        copy_w(0, 2, 0, "VS")
+        quant_w(0, 0, 1)
+        quant_x(0, 1)
+        head(2)
+        head_out(3, "S")
+        copy_w(0, 1, 1, "VS")
+        turn_x(0, 0)
+        head_out(2, "S")
+        x_out(0, 0, "S")
+        quant_w(0, 2, 1)
+        quant_w(0, 1, 1)
+        copy_w(0, 1, 0, "VV")
+        turn_x(1, 1)
+        head_out(4, "V")
+        turn_x(1, 0)
+        x_out(1, 1, "S")
+        quant_w(0, 1, 0)
+        turn_x(1, 2)
+        x_out(1, 0, "V")
+        quant_x(0, 0)
+        head_out(1, "S")
+        quant_w(0, 2, 0)
+        x_out(1, 2, "S")
+        quant_x(0, 2)
+        head(7)
+        copy_w(1, 2, 0, "VV")
+        copy_w(1, 2, 1, "SS")
+        head_out(7, "S")
+        quant_x(1, 1)
+        head(6)
+        quant_x(1, 0)
+        quant_w(1, 2, 0)
+        quant_x(1, 2)
+        head(5)
+        turn_x(2, 0)
+        head_out(6, "S")
+        turn_x(2, 1)
+        turn_x(2, 2)
+        copy_w(1, 0, 1, "VV")
+        head_out(5, "S")
+        quant_head(1)
+        narrow(0, 0, 0)
+        x_out(2, 2, "S")
+        narrow(1, 0, 0)
+        narrow(1, 0, 1)
+        copy_w(1, 1, 0, "VV")
+        copy_w(1, 0, 0, "SS")
+        narrow(3, 0, 0)
+        quant_w(1, 0, 0)
+        narrow(2, 0, 0)
+        narrow(0, 0, 1)
+        narrow(3, 0, 1)
+        quant_w(1, 1, 0)
+        narrow(2, 0, 1)
+        copy_w(1, 1, 1, "SS")
+        narrow(3, 1, 0)
+        quant_w(1, 0, 1)
+        narrow_out(0, 0, "S")
+        narrow_out(1, 0, "S")
+        quant_w(1, 1, 1)
+        x_out(2, 1, "S")
+        quant_w(1, 2, 1)
+        narrow(1, 1, 0)
         split_x(3)
-        for i in range(4):
-            quant_feat(i)
-        for n in range(2, PAIRS):
-            if n + 1 < PAIRS:
-                turn_x(n + 1)
-                x_out(n + 1, "SVS")
-            for h in range(H):
-                stage1(2 * n, h, range(4))
-                feat_out(2 * n, h)
-            if n + 1 < PAIRS:
-                quant_x(n + 1)
-            if n + 2 < PAIRS:
-                split_x(n + 2)
-            stage1(2 * n + 1, 0, range(4))
-            feat_out(2 * n + 1, 0)
-            quant_feat(2 * n)
-            stage1(2 * n + 1, 1, range(4))
-            feat_out(2 * n + 1, 1)
-            for i in range(0 if n == 2 else 2 * n - 2, 2 * n):
-                stage2(i)
-                if i == 2 * n - 2:
-                    quant_feat(2 * n + 1)
-        stage2(TILES - 2)
-        stage2(TILES - 1)
+        narrow(3, 1, 1)
+        x_out(2, 0, "S")
+        narrow_out(2, 0, "S")
+        narrow_out(3, 0, "V")
+        narrow(0, 1, 0)
+        narrow(1, 1, 1)
+        quant_x(2, 0)
+        narrow(0, 1, 1)
+        quant_x(2, 2)
+        narrow_out(3, 1, "S")
+        quant_x(2, 1)
+        turn_x(3, 1)
+        turn_x(3, 2)
+        turn_x(3, 0)
+        quant_feat(0, 0)
+        wide(2, 1, 0)
+        x_out(3, 0, "V")
+        wide(2, 0, 0)
+        narrow_out(1, 1, "S")
+        narrow_out(0, 1, "S")
+        quant_head(0)
+        x_out(3, 2, "S")
+        quant_x(3, 0)
+        x_out(3, 1, "S")
+        quant_feat(0, 1)
+        quant_x(3, 2)
+        wide_out(2, 1, 0, "V")
+        wide(2, 1, 1)
+        wide_out(2, 0, 0, "S")
+        wide(2, 0, 1)
+        narrow(2, 1, 0)
+        quant_feat(1, 0)
+        quant_x(3, 1)
+        multiply(0, 0)
+        split_x(4)
+        narrow(2, 1, 1)
+        narrow_out(2, 1, "S")
+        quant_feat(1, 1)
+        multiply(0, 1)
+        multiply(1, 0)
+        multiply(1, 1)
+        wide_out(2, 0, 1, "V")
+        turn_x(4, 1)
+        turn_x(4, 2)
+        turn_x(4, 0)
+        wide_out(2, 1, 1, "S")
+        wide(3, 1, 0)
+        x_out(4, 0, "V")
+        wide(3, 0, 0)
+        multiply(2, 0)
+        subtract(0)
+        x_out(4, 2, "S")
+        quant_x(4, 0)
+        multiply(2, 1)
+        x_out(4, 1, "S")
+        quant_x(4, 2)
+        wide_out(3, 1, 0, "S")
+        subtract(1)
+        quant_feat(2, 1)
+        wide(3, 1, 1)
+        wide_out(3, 0, 0, "S")
+        wide(3, 0, 1)
+        quant_x(4, 1)
+        split_x(5)
+        multiply(3, 0)
+        subtract(2)
+        square(2)
+        quant_feat(2, 0)
+        multiply(3, 1)
+        wide_out(3, 0, 1, "V")
+        turn_x(5, 1)
+        turn_x(5, 2)
+        turn_x(5, 0)
+        wide_out(3, 1, 1, "S")
+        wide(4, 1, 0)
+        x_out(5, 0, "V")
+        wide(4, 0, 0)
+        multiply(4, 0)
+        x_out(5, 2, "S")
+        quant_x(5, 0)
+        multiply(4, 1)
+        subtract(3)
+        x_out(5, 1, "S")
+        quant_x(5, 2)
+        wide_out(4, 1, 0, "S")
+        quant_feat(3, 1)
+        wide(4, 1, 1)
+        wide_out(4, 0, 0, "S")
+        wide(4, 0, 1)
+        quant_x(5, 1)
+        split_x(6)
+        square(1)
+        multiply(5, 0)
+        subtract(4)
+        store(0)
+        square(3)
+        square(0)
+        square(4)
+        quant_feat(3, 0)
+        multiply(5, 1)
+        wide_out(4, 0, 1, "V")
+        turn_x(6, 1)
+        store(1)
+        turn_x(6, 2)
+        turn_x(6, 0)
+        wide_out(4, 1, 1, "S")
+        wide(5, 1, 0)
+        x_out(6, 0, "V")
+        wide(5, 0, 0)
+        multiply(6, 0)
+        x_out(6, 2, "S")
+        quant_x(6, 0)
+        multiply(6, 1)
+        subtract(5)
+        x_out(6, 1, "S")
+        quant_x(6, 2)
+        wide_out(5, 1, 0, "S")
+        quant_feat(4, 1)
+        wide(5, 1, 1)
+        wide_out(5, 0, 0, "S")
+        wide(5, 0, 1)
+        quant_x(6, 1)
+        split_x(7)
+        multiply(7, 0)
+        subtract(6)
+        square(5)
+        square(6)
+        quant_feat(4, 0)
+        multiply(7, 1)
+        wide_out(5, 0, 1, "V")
+        turn_x(7, 1)
+        store(2)
+        turn_x(7, 2)
+        turn_x(7, 0)
+        wide_out(5, 1, 1, "S")
+        wide(6, 1, 0)
+        x_out(7, 0, "V")
+        wide(6, 0, 0)
+        multiply(8, 0)
+        x_out(7, 2, "S")
+        quant_x(7, 0)
+        multiply(8, 1)
+        subtract(7)
+        x_out(7, 1, "S")
+        quant_x(7, 2)
+        wide_out(6, 1, 0, "S")
+        quant_feat(5, 1)
+        wide(6, 1, 1)
+        wide_out(6, 0, 0, "S")
+        wide(6, 0, 1)
+        quant_x(7, 1)
+        multiply(9, 0)
+        subtract(8)
+        narrow(14, 0, 0)
+        square(7)
+        narrow(14, 1, 0)
+        narrow(14, 0, 1)
+        square(8)
+        quant_feat(5, 0)
+        multiply(9, 1)
+        narrow(14, 1, 1)
+        wide_out(6, 0, 1, "V")
+        store(3)
+        wide_out(6, 1, 1, "S")
+        narrow_out(14, 1, "S")
+        multiply(10, 0)
+        multiply(10, 1)
+        narrow(15, 1, 0)
+        subtract(9)
+        narrow_out(14, 0, "S")
+        quant_feat(6, 1)
+        narrow(15, 1, 1)
+        multiply(11, 0)
+        subtract(10)
+        square(9)
+        quant_feat(7, 1, 0)
+        narrow_out(15, 1, "B")
+        quant_feat(7, 0, 0)
+        narrow(15, 0, 0)
+        square(10)
+        quant_feat(6, 0)
+        narrow(15, 0, 1)
+        multiply(11, 1)
+        store(4)
+        quant_feat(7, 1, 1)
+        multiply(12, 0)
+        multiply(12, 1)
+        multiply(14, 0)
+        narrow_out(15, 0, "S")
+        subtract(11)
+        quant_feat(7, 0, 1)
+        multiply(13, 0)
+        subtract(12)
+        square(11)
+        multiply(14, 1)
+        square(12)
+        multiply(13, 1)
+        multiply(15, 0)
+        store(5)
+        subtract(14)
+        subtract(13)
+        multiply(15, 1)
+        square(14)
+        square(13)
+        store(7, 0)
+        subtract(15)
+        store(6)
+        store(7, 1)
+        square(15)
         nc.sync.dma_start(out=out_1.rearrange("(p i) -> p i", i=TILES), in_=score[:])

from contextlib import ExitStack

import concourse.mybir as mybir
from concourse.masks import make_identity

M, K, D, R, C = 2048, 1536, 1024, 1024, 512
FLOPS = 2 * (M * K * D + D * R * C + M * D * C)

F32 = mybir.dt.float32
BF16 = mybir.dt.bfloat16
I32 = mybir.dt.int32
U32 = mybir.dt.uint32
U8 = mybir.dt.uint8
FP8 = mybir.dt.float8_e4m3fn_x4
FP4 = mybir.dt.float4_e2m1fn_x4
RELU = mybir.ActivationFunctionType.Relu
SQUARE = mybir.ActivationFunctionType.Square
SUB = mybir.AluOpType.subtract

P = 128
GX = K // 512
GR = R // 512
H = D // 512
TILES = M // P
PAIRS = TILES // 2
FIRST = 3


def tile_el2n_pruning_score_s12_kernel(tc, x, w, u_words, u_scales, v_words, v_scales, y, out_0, out_1):
    nc = tc.nc
    with ExitStack() as ctx:
        keep = ctx.enter_context(tc.tile_pool(name="keep", bufs=1))
        work = ctx.enter_context(tc.tile_pool(name="work", bufs=3))
        psum = ctx.enter_context(tc.psum_pool(name="psum", bufs=5))
        ctx.enter_context(tc.manual_schedule())

        ident = keep.tile([P, P], F32, name="ident")
        make_identity(nc, ident[:])
        zeros = keep.tile([P, C], BF16, name="zeros", align_bytes=64)
        nc.gpsimd.memset(zeros[:], 0.0)
        u_plane = keep.tile([P, GR, D], U8, name="u_plane", align_bytes=64)
        v_plane = keep.tile([P, GR, C], U8, name="v_plane", align_bytes=64)
        nc.vector.memset(v_plane[:].bitcast(I32), 0)
        nc.vector.memset(u_plane[:].bitcast(I32), 0)
        warm = keep.tile([P, 1], F32, name="warm")
        nc.vector.memset(warm[:], 0.0)
        warm2 = keep.tile([P, 1], F32, name="warm2")

        u_raw = keep.tile([P, GR, 2 * D], U8, name="u_raw", align_bytes=64)
        v_raw = keep.tile([P, GR, 2 * C], U8, name="v_raw", align_bytes=64)
        us = u_scales.bitcast(I32).rearrange("g q n -> q g n")
        vs = v_scales.bitcast(I32).rearrange("g q n -> q g n")
        def load_scales(queue, plane, rows, qs):
            for q in qs:
                queue.dma_start(out=plane[32 * q : 32 * q + 4].bitcast(I32), in_=rows[4 * q : 4 * q + 4])

        x_rows = x.rearrange("(p i) k -> p i k", i=TILES)
        y_rows = y.rearrange("(p i) c -> p i c", i=TILES)
        out_rows = out_0.rearrange("(p i) c -> p i c", i=TILES)
        w_rows = w.rearrange("(g p j) d -> g p j d", p=P, j=4)

        x_raw = [keep.tile([P, 2, K], BF16, name=f"x_raw{n}", align_bytes=64) for n in range(PAIRS)]
        y_sb = [keep.tile([P, 4, C], BF16, name=f"y_sb{n}", align_bytes=64) for n in range(TILES // 4)]
        w_raw = [[keep.tile([P, 4, 512], BF16, name=f"w_raw{h}{g}", align_bytes=64) for g in range(GX)] for h in range(H)]

        def load_w(h, g):
            nc.sync.dma_start(out=w_raw[h][g][:], in_=w_rows[g][:, :, 512 * h : 512 * h + 512])

        def load_x(n):
            nc.sync.dma_start(out=x_raw[n][:], in_=x_rows[:, 2 * n : 2 * n + 2, :])

        def load_y(n):
            nc.sync.dma_start(out=y_sb[n][:], in_=y_rows[:, 4 * n : 4 * n + 4, :])

        load_scales(nc.gpsimd, v_plane, vs, (2, 3))
        load_scales(nc.scalar, v_plane, vs, (0, 1))
        load_scales(nc.scalar, u_plane, us, (0, 1, 2, 3))
        nc.scalar.activation(out=warm2[:], in_=warm[:], func=RELU)
        load_w(0, 0)
        nc.sync.dma_start(out=u_raw[:].bitcast(I32), in_=u_words.bitcast(I32).rearrange("g p n -> p g n"))
        load_x(0)
        nc.sync.dma_start(out=v_raw[:].bitcast(I32), in_=v_words.bitcast(I32).rearrange("g p n -> p g n"))
        load_w(0, 2)
        load_w(0, 1)
        load_x(1)
        load_w(1, 2)
        load_x(2)
        load_w(1, 0)
        load_w(1, 1)
        load_y(0)
        load_x(3)
        load_x(4)
        load_y(1)
        load_x(5)
        load_x(6)
        load_y(2)
        load_x(7)
        load_y(3)

        u_codes = keep.tile([P, GR, 2 * D], U8, name="u_codes", align_bytes=64)
        u_perm = keep.tile([P, GR, D], U8, name="u_perm", align_bytes=64)

        def order_codes(g):
            nc.vector.tensor_copy(
                out=u_codes[:, g, :].bitcast(I32).rearrange("p (t q b) -> p t q b", t=4, b=2),
                in_=u_raw[:, g, :].bitcast(I32).rearrange("p (q t b) -> p t q b", t=4, b=2),
            )

        def order_scales(g):
            nc.vector.tensor_copy(
                out=u_perm[:, g, :].bitcast(I32).rearrange("p (t q) -> p t q", t=4),
                in_=u_plane[:, g, :].bitcast(I32).rearrange("p (q t) -> p t q", t=4),
            )

        head_bf = keep.tile([P, H, 4 * C], BF16, name="head_bf", align_bytes=64)
        head_codes = keep.tile([P, H, C], U32, name="head_codes", align_bytes=64)
        head_scales = keep.tile([P, H, C], U8, name="head_scales", align_bytes=64)
        banks = {}

        def head(n):
            h, cc = divmod(n, 4)
            acc = psum.tile([P, 4, P], F32, name="acc", tag="acc", bufs=5)
            for t in range(4):
                col = 256 * t + 128 * h
                for g in range(GR):
                    nc.tensor.matmul_mx(
                        out=acc[:, t, :],
                        lhsT=u_codes[:, g, 2 * col : 2 * col + 256].bitcast(FP4),
                        lhsT_scale=u_perm[:, g, col : col + 128],
                        rhs=v_raw[:, g, 256 * cc : 256 * cc + 256].bitcast(FP4),
                        rhs_scale=v_plane[:, g, 128 * cc : 128 * cc + 128],
                        start=(g == 0),
                        stop=(g == GR - 1),
                    )
            banks["head", n] = acc

        def copy_out(engine, dst, src):
            if engine == "S":
                nc.scalar.copy(out=dst, in_=src)
            else:
                nc.vector.tensor_copy(out=dst, in_=src)

        def head_out(n, engine="S"):
            h, cc = divmod(n, 4)
            dst = head_bf[:, h, 512 * cc : 512 * cc + 512].rearrange("p (c t) -> p c t", t=4)
            copy_out(engine, dst, banks["head", n][:].rearrange("p t c -> p c t"))

        def quant_head(h):
            nc.vector.quantize_mx(
                out=head_codes[:, h, :].bitcast(FP8), scales=head_scales[:, h, :], in_=head_bf[:, h, :]
            )

        w_bf = [[keep.tile([P, 2048], BF16, name=f"w_bf{h}{g}", align_bytes=64) for g in range(GX)] for h in range(H)]
        w_codes = [[keep.tile([P, 512], U32, name=f"w_codes{h}{g}", align_bytes=64) for g in range(GX)] for h in range(H)]
        w_scales = [[keep.tile([P, 512], U8, name=f"w_scales{h}{g}", align_bytes=64) for g in range(GX)] for h in range(H)]

        def copy_w(h, g, half, engines):
            src = w_raw[h][g][:].rearrange("p j (q t b) -> p t q j b", t=4, b=4)
            dst = w_bf[h][g][:].rearrange("p (t q b j) -> p t q j b", t=4, b=4, j=4)
            t = 2 * half
            if engines == "VV":
                nc.vector.tensor_copy(out=dst[:, t : t + 2], in_=src[:, t : t + 2])
            else:
                copy_out(engines[0], dst[:, t], src[:, t])
                copy_out(engines[1], dst[:, t + 1], src[:, t + 1])

        def quant_w(h, g, half):
            nc.vector.quantize_mx(
                out=w_codes[h][g][:, 256 * half : 256 * half + 256].bitcast(FP8),
                scales=w_scales[h][g][:, 256 * half : 256 * half + 256],
                in_=w_bf[h][g][:, 1024 * half : 1024 * half + 1024],
            )

        x_split = {}
        x_bf = {}
        x_codes = {}
        x_scales = {}

        def split_x(n):
            xs = work.tile([P, 2, 2, K // 4], F32, name="x_split", align_bytes=64)
            nc.vector.tensor_copy(out=xs[:], in_=x_raw[n][:].bitcast(F32).rearrange("p i (w u) -> p i u w", u=2))
            x_split[n] = xs

        def turn_x(n, g):
            words = x_raw[n][:].bitcast(F32)
            tp = psum.tile([P, 2, 2, P], F32, name="tp", tag="tp", bufs=3)
            for i in range(2):
                for u in range(2):
                    if n < FIRST:
                        src = words[:, i, 256 * g + u : 256 * g + 256 : 2]
                    else:
                        src = x_split[n][:, i, u, 128 * g : 128 * g + 128]
                    nc.tensor.transpose(tp[:, i, u, :], src, ident[:])
            banks["x", n, g] = tp

        def x_out(n, g, engine):
            if n not in x_bf:
                x_bf[n] = work.tile([P, 6 * 512], BF16, name="x_bf", align_bytes=64)
            dst = x_bf[n][:, 1024 * g : 1024 * g + 1024].bitcast(F32).rearrange("p (i m u) -> p i m u", i=2, u=2)
            copy_out(engine, dst, banks["x", n, g][:].rearrange("p i u m -> p i m u"))

        def quant_x(n, g):
            if n not in x_codes:
                x_codes[n] = work.tile([P, 6 * 128], U32, name="x_codes", align_bytes=64)
                x_scales[n] = work.tile([P, 6 * 128], U8, name="x_scales", align_bytes=64)
            nc.vector.quantize_mx(
                out=x_codes[n][:, 256 * g : 256 * g + 256].bitcast(FP8),
                scales=x_scales[n][:, 256 * g : 256 * g + 256],
                in_=x_bf[n][:, 1024 * g : 1024 * g + 1024],
            )

        feat_bf = {}
        feat_codes = {}
        feat_scales = {}

        def open_feat(n):
            if n not in feat_bf:
                feat_bf[n] = work.tile([P, H, 1024], BF16, name="feat_bf", bufs=3, align_bytes=64)

        def passes(acc, n, h, t, cols):
            for g in range(GX):
                at = slice(256 * g + cols.start, 256 * g + cols.stop)
                nc.tensor.matmul_mx(
                    out=acc,
                    lhsT=w_codes[h][g][:, 128 * t : 128 * t + 128].bitcast(FP8),
                    lhsT_scale=w_scales[h][g][:, 128 * t : 128 * t + 128],
                    rhs=x_codes[n][:, at].bitcast(FP8),
                    rhs_scale=x_scales[n][:, at],
                    start=(g == 0),
                    stop=(g == GX - 1),
                )

        def narrow(i, h, half):
            n, k = divmod(i, 2)
            if ("feat", i, h) not in banks:
                banks["feat", i, h] = psum.tile([P, 4, P], F32, name="acc", tag="acc", bufs=5)
            for t in (2 * half, 2 * half + 1):
                passes(banks["feat", i, h][:, t, :], n, h, t, slice(128 * k, 128 * k + 128))

        def relu_out(engine, dst, src):
            if engine == "S":
                nc.scalar.activation(out=dst, in_=src, func=RELU)
            else:
                nc.vector.tensor_scalar_max(out=dst, in0=src, scalar1=0.0)

        def narrow_out(i, h, engine):
            n, k = divmod(i, 2)
            open_feat(n)
            dst = feat_bf[n][:, h, 512 * k : 512 * k + 512].rearrange("p (m t) -> p m t", t=4)
            src = banks["feat", i, h][:].rearrange("p t m -> p m t")
            if engine == "B":
                relu_out("S", dst[:, 0:64], src[:, 0:64])
                relu_out("V", dst[:, 64:128], src[:, 64:128])
            else:
                relu_out(engine, dst, src)

        def wide(n, h, half):
            acc = psum.tile([P, 2, 256], F32, name="acc", tag="acc", bufs=5)
            for tt in range(2):
                passes(acc[:, tt, :], n, h, 2 * half + tt, slice(0, 256))
            banks["wide", n, h, half] = acc

        def wide_out(n, h, half, engine):
            open_feat(n)
            dst = feat_bf[n][:, h, :].rearrange("p (m t) -> p m t", t=4)[:, :, 2 * half : 2 * half + 2]
            relu_out(engine, dst, banks["wide", n, h, half][:].rearrange("p t m -> p m t"))

        def quant_feat(n, h, k=None):
            if n not in feat_codes:
                feat_codes[n] = work.tile([P, H, 256], U32, name="feat_codes", bufs=3, align_bytes=64)
                feat_scales[n] = work.tile([P, H, 256], U8, name="feat_scales", bufs=3, align_bytes=64)
            rows = slice(0, 256) if k is None else slice(128 * k, 128 * k + 128)
            nc.vector.quantize_mx(
                out=feat_codes[n][:, h, rows].bitcast(FP8),
                scales=feat_scales[n][:, h, rows],
                in_=feat_bf[n][:, h, 4 * rows.start : 4 * rows.stop],
            )

        score = keep.tile([P, TILES], F32, name="score")
        err = {}

        def multiply(i, h):
            n, k = divmod(i, 2)
            if h == 0:
                banks["res", i] = psum.tile([P, C], F32, name="res", tag="acc", bufs=5)
            nc.tensor.matmul_mx(
                out=banks["res", i][:],
                lhsT=feat_codes[n][:, h, 128 * k : 128 * k + 128].bitcast(FP8),
                lhsT_scale=feat_scales[n][:, h, 128 * k : 128 * k + 128],
                rhs=head_codes[:, h, :].bitcast(FP8),
                rhs_scale=head_scales[:, h, :],
                start=(h == 0),
                stop=(h == H - 1),
            )

        def subtract(i):
            n, k = divmod(i, 2)
            if n not in err:
                err[n] = work.tile([P, 2, C], F32, name="err", align_bytes=64)
            nc.vector.tensor_tensor(out=err[n][:, k, :], in0=banks["res", i][:], in1=y_sb[i // 4][:, i % 4, :], op=SUB)

        def square(i):
            n, k = divmod(i, 2)
            junk = work.tile([P, C], BF16, name="junk", bufs=2)
            nc.scalar.activation(
                out=junk[:], in_=err[n][:, k, :], func=SQUARE, scale=1.0 / C**0.5, accum_out=score[:, i : i + 1]
            )

        def store(n, k=None):
            if k is None:
                nc.sync.dma_start(out=out_rows[:, 2 * n : 2 * n + 2, :], in_=err[n][:])
            else:
                nc.sync.dma_start(out=out_rows[:, 2 * n + k, :], in_=err[n][:, k, :])

        for n in range(8):
            dummy = psum.tile([P, C], F32, name="dummy", tag="tp", bufs=3)
            nc.tensor.matmul(dummy[:], lhsT=zeros[:, 0:128], rhs=zeros[:], start=True, stop=True)
        copy_w(0, 0, 0, "SS")
        order_codes(1)
        turn_x(0, 2)
        order_codes(0)
        order_scales(0)
        copy_w(0, 0, 1, "VS")
        x_out(0, 2, "S")
        order_scales(1)
        quant_w(0, 0, 0)
        turn_x(0, 1)
        head(0)
        head(3)
        x_out(0, 1, "S")
        head_out(0, "V")
        head(1)
        copy_w(0, 2, 1, "VS")
        head(4)
        copy_w(0, 2, 0, "VS")
        quant_w(0, 0, 1)
        quant_x(0, 1)
        head(2)
        head_out(3, "S")
        copy_w(0, 1, 1, "VS")
        turn_x(0, 0)
        head_out(2, "S")
        x_out(0, 0, "S")
        quant_w(0, 2, 1)
        quant_w(0, 1, 1)
        copy_w(0, 1, 0, "VV")
        turn_x(1, 1)
        head_out(4, "V")
        turn_x(1, 0)
        x_out(1, 1, "S")
        quant_w(0, 1, 0)
        turn_x(1, 2)
        x_out(1, 0, "V")
        quant_x(0, 0)
        head_out(1, "S")
        quant_w(0, 2, 0)
        x_out(1, 2, "S")
        quant_x(0, 2)
        head(7)
        copy_w(1, 2, 0, "VV")
        copy_w(1, 2, 1, "SS")
        head_out(7, "S")
        quant_x(1, 1)
        head(6)
        quant_x(1, 0)
        quant_w(1, 2, 0)
        quant_x(1, 2)
        head(5)
        turn_x(2, 0)
        head_out(6, "S")
        turn_x(2, 1)
        turn_x(2, 2)
        copy_w(1, 0, 1, "VV")
        head_out(5, "S")
        quant_head(1)
        narrow(0, 0, 0)
        x_out(2, 2, "S")
        narrow(1, 0, 0)
        narrow(1, 0, 1)
        copy_w(1, 1, 0, "VV")
        copy_w(1, 0, 0, "SS")
        narrow(3, 0, 0)
        quant_w(1, 0, 0)
        narrow(2, 0, 0)
        narrow(0, 0, 1)
        narrow(3, 0, 1)
        quant_w(1, 1, 0)
        narrow(2, 0, 1)
        copy_w(1, 1, 1, "SS")
        narrow(3, 1, 0)
        quant_w(1, 0, 1)
        narrow_out(0, 0, "S")
        narrow_out(1, 0, "S")
        quant_w(1, 1, 1)
        x_out(2, 1, "S")
        quant_w(1, 2, 1)
        narrow(1, 1, 0)
        split_x(3)
        narrow(3, 1, 1)
        x_out(2, 0, "S")
        narrow_out(2, 0, "S")
        narrow_out(3, 0, "V")
        narrow(0, 1, 0)
        narrow(1, 1, 1)
        quant_x(2, 0)
        narrow(0, 1, 1)
        quant_x(2, 2)
        narrow_out(3, 1, "S")
        quant_x(2, 1)
        turn_x(3, 1)
        turn_x(3, 2)
        turn_x(3, 0)
        quant_feat(0, 0)
        wide(2, 1, 0)
        x_out(3, 0, "V")
        wide(2, 0, 0)
        narrow_out(1, 1, "S")
        narrow_out(0, 1, "S")
        quant_head(0)
        x_out(3, 2, "S")
        quant_x(3, 0)
        x_out(3, 1, "S")
        quant_feat(0, 1)
        quant_x(3, 2)
        wide_out(2, 1, 0, "V")
        wide(2, 1, 1)
        wide_out(2, 0, 0, "S")
        wide(2, 0, 1)
        narrow(2, 1, 0)
        quant_feat(1, 0)
        quant_x(3, 1)
        multiply(0, 0)
        split_x(4)
        narrow(2, 1, 1)
        narrow_out(2, 1, "S")
        quant_feat(1, 1)
        multiply(0, 1)
        multiply(1, 0)
        multiply(1, 1)
        wide_out(2, 0, 1, "V")
        turn_x(4, 1)
        turn_x(4, 2)
        turn_x(4, 0)
        wide_out(2, 1, 1, "S")
        wide(3, 1, 0)
        x_out(4, 0, "V")
        wide(3, 0, 0)
        multiply(2, 0)
        subtract(0)
        x_out(4, 2, "S")
        quant_x(4, 0)
        multiply(2, 1)
        x_out(4, 1, "S")
        quant_x(4, 2)
        wide_out(3, 1, 0, "S")
        subtract(1)
        quant_feat(2, 1)
        wide(3, 1, 1)
        wide_out(3, 0, 0, "S")
        wide(3, 0, 1)
        quant_x(4, 1)
        split_x(5)
        multiply(3, 0)
        subtract(2)
        square(2)
        quant_feat(2, 0)
        multiply(3, 1)
        wide_out(3, 0, 1, "V")
        turn_x(5, 1)
        turn_x(5, 2)
        turn_x(5, 0)
        wide_out(3, 1, 1, "S")
        wide(4, 1, 0)
        x_out(5, 0, "V")
        wide(4, 0, 0)
        multiply(4, 0)
        x_out(5, 2, "S")
        quant_x(5, 0)
        multiply(4, 1)
        subtract(3)
        x_out(5, 1, "S")
        quant_x(5, 2)
        wide_out(4, 1, 0, "S")
        quant_feat(3, 1)
        wide(4, 1, 1)
        wide_out(4, 0, 0, "S")
        wide(4, 0, 1)
        quant_x(5, 1)
        split_x(6)
        square(1)
        multiply(5, 0)
        subtract(4)
        store(0)
        square(3)
        square(0)
        square(4)
        quant_feat(3, 0)
        multiply(5, 1)
        wide_out(4, 0, 1, "V")
        turn_x(6, 1)
        store(1)
        turn_x(6, 2)
        turn_x(6, 0)
        wide_out(4, 1, 1, "S")
        wide(5, 1, 0)
        x_out(6, 0, "V")
        wide(5, 0, 0)
        multiply(6, 0)
        x_out(6, 2, "S")
        quant_x(6, 0)
        multiply(6, 1)
        subtract(5)
        x_out(6, 1, "S")
        quant_x(6, 2)
        wide_out(5, 1, 0, "S")
        quant_feat(4, 1)
        wide(5, 1, 1)
        wide_out(5, 0, 0, "S")
        wide(5, 0, 1)
        quant_x(6, 1)
        split_x(7)
        multiply(7, 0)
        subtract(6)
        square(5)
        square(6)
        quant_feat(4, 0)
        multiply(7, 1)
        wide_out(5, 0, 1, "V")
        turn_x(7, 1)
        store(2)
        turn_x(7, 2)
        turn_x(7, 0)
        wide_out(5, 1, 1, "S")
        wide(6, 1, 0)
        x_out(7, 0, "V")
        wide(6, 0, 0)
        multiply(8, 0)
        x_out(7, 2, "S")
        quant_x(7, 0)
        multiply(8, 1)
        subtract(7)
        x_out(7, 1, "S")
        quant_x(7, 2)
        wide_out(6, 1, 0, "S")
        quant_feat(5, 1)
        wide(6, 1, 1)
        wide_out(6, 0, 0, "S")
        wide(6, 0, 1)
        quant_x(7, 1)
        multiply(9, 0)
        subtract(8)
        narrow(14, 0, 0)
        square(7)
        narrow(14, 1, 0)
        narrow(14, 0, 1)
        square(8)
        quant_feat(5, 0)
        multiply(9, 1)
        narrow(14, 1, 1)
        wide_out(6, 0, 1, "V")
        store(3)
        wide_out(6, 1, 1, "S")
        narrow_out(14, 1, "S")
        multiply(10, 0)
        multiply(10, 1)
        narrow(15, 1, 0)
        subtract(9)
        narrow_out(14, 0, "S")
        quant_feat(6, 1)
        narrow(15, 1, 1)
        multiply(11, 0)
        subtract(10)
        square(9)
        quant_feat(7, 1, 0)
        narrow_out(15, 1, "B")
        quant_feat(7, 0, 0)
        narrow(15, 0, 0)
        square(10)
        quant_feat(6, 0)
        narrow(15, 0, 1)
        multiply(11, 1)
        store(4)
        quant_feat(7, 1, 1)
        multiply(12, 0)
        multiply(12, 1)
        multiply(14, 0)
        narrow_out(15, 0, "S")
        subtract(11)
        quant_feat(7, 0, 1)
        multiply(13, 0)
        subtract(12)
        square(11)
        multiply(14, 1)
        square(12)
        multiply(13, 1)
        multiply(15, 0)
        store(5)
        subtract(14)
        subtract(13)
        multiply(15, 1)
        square(14)
        square(13)
        store(7, 0)
        subtract(15)
        store(6)
        store(7, 1)
        square(15)
        nc.sync.dma_start(out=out_1.rearrange("(p i) -> p i", i=TILES), in_=score[:])
